import numpy as np, ml_dtypes
CORES = [24,48,72,152,176,200]
N = 6
import mx_ref
NC, G = 128, 2
C, C2 = np.float32(0.043), np.float32(0.01755)
BF = ml_dtypes.bfloat16
def cut(t, i, w=512):
    return t[:, w * i:w * i + w]
def tile(rs):
    return np.stack(rs, axis=2).reshape(128, -1).astype(BF)
def layer(w, X):
    out = []
    for i in range(G):
        for t in range(len(X)):
            p = mx_ref.matmul(mx_ref.quantize(cut(w, len(X) * i + t)), X[t])
            z = p if t == 0 else z + p
        out.append(z)
    return out
def act(Z):
    return [np.maximum(s * z, 0) * C for z in Z for s in (1, -1)]
def act2(Z):
    return [np.maximum(s * z, 0) * C2 for z in Z for s in (1, -1)]
def setup_inputs(rng):
    def f(*shape):
        return mx_ref.flush((rng.standard_normal(shape, dtype=np.float32) * np.exp2(rng.integers(-2, 3, shape[:-1] + (1,)))).astype(BF))
    return {"x": f(N, 128, 4 * NC), "w1": f(N, 128, G * 512), "w2": f(N, 128, G * 512), "w3": f(N, 128, G * 512), "w4": f(N, 128, 512)}
def setup_inputs_blocks(rng):
    d = setup_inputs(rng)
    for k in ("x", "w1", "w2", "w3", "w4"): d[k] = mx_ref.spread(d[k], rng, 2)
    return d
def setup_inputs_wide(rng):
    d = setup_inputs(rng)
    for k in ("x", "w1", "w2", "w3", "w4"): d[k] = mx_ref.flush((d[k].astype(np.float32) * np.exp2(rng.integers(-4, 5, (N, 1, 1))).astype(np.float32)).astype(BF))
    return d
def reference(x, w1, w2, w3, w4, own=None):
    X = [mx_ref.quantize(x[j]) for j in range(N)]
    t = np.stack([np.stack([tile(act(layer(w1[r], [X[c]]))) for c in range(N)]) for r in range(N)])
    uset = t if own is None else own["t"]
    h = np.zeros((N, 128, 4 * NC), BF)
    for c in range(N):
        for r in range(N):
            P = layer(w2[r], [mx_ref.quantize(uset[r][c])])
            Z = P if r == 0 else [z + p for z, p in zip(Z, P)]
        h[c] = tile(act2(Z))
    use = h if own is None else own["h"]
    H = [mx_ref.quantize(use[j]) for j in range(N)]
    y = np.zeros((N, 128, NC), np.float32)
    for c in range(N):
        for r in range(N):
            p = mx_ref.matmul(mx_ref.quantize(w4[r]), mx_ref.quantize(tile(act(layer(w3[r], [H[c]])))))
            y[c] = p if r == 0 else y[c] + p
    return {"t": t, "h": h, "y": y}

import numpy as np
from concourse.bass import DstId, RemoteDMATransfer
from concourse.mybir import dt, AluOpType, ActivationFunctionType

N = 6
C1 = float(np.float32(0.043))
C2 = float(np.float32(0.01755))
F8, U8, F32, BF16 = "float8_e4m3fn_x4", "uint8", "float32", "bfloat16"

TILES = ({False: "nn|ffn", True: "n|ffff"}, {False: "ffnnn", True: "ffffn"})
SUMS = ({False: "nnnff", True: "nffff"}, {False: "nnfnf", True: "nffff"})

SCRATCH = {
    "xb": ("sbuf", [128, 512], BF16),
    "w1b": ("sbuf", [128, 1024], BF16),
    "w2b": ("sbuf", [128, 1024], BF16),
    "w3b": ("sbuf", [128, 1024], BF16),
    "w4b": ("sbuf", [128, 512], BF16),
    "w1c": ("sbuf", [128, 256], F8), "w1p": ("sbuf", [128, 256], U8),
    "w2c": ("sbuf", [128, 256], F8), "w2p": ("sbuf", [128, 256], U8),
    "w3c": ("sbuf", [128, 256], F8), "w3p": ("sbuf", [128, 256], U8),
    "w4c": ("sbuf", [128, 128], F8), "w4p": ("sbuf", [128, 128], U8),
    "xc": ("sbuf", [128, 128 * N], F8), "xp": ("sbuf", [128, 128 * N], U8),
    "hc": ("sbuf", [128, 128 * N], F8), "hp": ("sbuf", [128, 128 * N], U8),
    "tb": ("sbuf", [128, 512 * N], BF16),
    "tc": ("sbuf", [128, 128 * N], F8), "tp": ("sbuf", [128, 128 * N], U8),
    "ub": ("sbuf", [128, 512 * N], BF16),
    "uc": ("sbuf", [128, 128 * N], F8), "up": ("sbuf", [128, 128 * N], U8),
    "so": ("sbuf", [128, 256 * N], F32), "sl": ("sbuf", [128, 256 * N], F32),
    "yo": ("sbuf", [128, 128 * N], F32), "yl": ("sbuf", [128, 128 * N], F32),
    "acc": ("sbuf", [128, 256], F32),
    "hb": ("sbuf", [128, 512], BF16),
    "yacc": ("sbuf", [128, 128], F32),
    "ps": ("psum", [128, 4096], F32),
}
PIECES = ("xp", "xc", "sA", "sB", "hp", "hc", "y")
CUT = {"s": (0, 256), "sA": (0, 128), "sB": (128, 256)}
SEMAPHORES = [p + str(r) for p in PIECES + ("s",) for r in range(N)] + [
    "ldx", "ldw1", "ldw2", "ldw34", "qx", "qw1", "qw2", "qw34", "qh", "va", "vh", "sh", "vy",
    "z0a", "z1a", "va1", "sa1", "qt", "p0a", "p1a", "cv1", "cs1",
    "z0b", "z1b", "va2", "sa2", "qu", "p0b", "cs2",
    "lx", "ls", "lh", "ly", "st", "rl",
]


def bits(m):
    return bin(m).count("1")


def same_chip(topo, a, b):
    return topo.host(a) == topo.host(b) and topo.chip(a) == topo.chip(b)


def roads(T, topo):
    cores = T.cores
    plane = [[c for c in range(N) if c != r and topo.same_plane(cores[r], cores[c])] for r in range(N)]
    other = [[c for c in range(N) if c != r and c not in plane[r]] for r in range(N)]
    sims = range(2 * 128)
    used, relay = set(cores), {}
    for r in range(N):
        src = cores[r]
        mine = sorted(plane[r] + [r]).index(r)
        for j, c in enumerate(other[r]):
            dst = cores[c]
            swap = (mine + j) % 2 == 1
            if len(other[r]) > len(plane[r]) and swap:
                cand = [k for k in sims if topo.mates(k, dst) and topo.may_write(src, k) and topo.may_write(k, dst)
                        and topo.die(k) == topo.die(src)]
            else:
                far = swap if len(other[r]) <= len(plane[r]) else True
                cand = [k for k in sims if same_chip(topo, k, src) and topo.may_write(k, dst)
                        and (topo.die(k) != topo.die(src)) == far]
            k = [k for k in cand if k not in used][0]
            used.add(k)
            relay[(r, c)] = k
    return plane, other, relay


def turn(lst, r, sign):
    return sorted(lst, key=lambda c: (sign * (c - r)) % N)


def mix(pattern, near, far):
    left = {"n": list(near), "f": list(far)}
    return [left[ch].pop(0) for ch in pattern if ch in left]


def steps(pattern):
    events, k, waiting = [("Z", 0), ("P", 0)], 0, None
    for ch in pattern + "|":
        if ch != "|":
            k += 1
            events.append(("Z", k))
        if waiting is not None:
            events.append(("P", waiting))
        waiting = None if ch == "|" else k
    return events


def slot(t, r, w):
    return t[:, w * r:w * r + w]


def piece(T, p, r, out):
    if p in ("xc", "hc"):
        return T[p][:, 128 * r:128 * r + 128].bitcast(dt.uint8)
    if p in ("xp", "hp"):
        return T[p][:, 128 * r:128 * r + 128]
    if p in CUT:
        return (T.so if out else T.sl)[:, 256 * r + CUT[p][0]:256 * r + CUT[p][1]]
    return slot(T.yo if out else T.yl, r, 128)


def relay_program(g, core, T, topo, r, dst):
    rid, pid = topo.addr(dst, core)
    m = topo.mask(core, dst)
    n = 0
    for p in PIECES:
        g.wait_ge(T.sem[p + str(r)], bits(m))
        g.remote_dma(piece(T, p, r, False), piece(T, p, r, False), T.sem[p + str(r)], T.sem.rl, pid, rid, m)
        n += bits(m)
    g.wait_ge(T.sem.rl, n)


def rank_program(g, core, T, topo):
    plane, other, relay = roads(T, topo)
    me = T.rank_of(core)
    if me is None:
        for (r, c), k in relay.items():
            if k == core:
                relay_program(g, core, T, topo, r, T.cores[c])
        return
    sem, cores = T.sem, T.cores
    hop = {c: relay.get((me, c), cores[c]) for c in range(N) if c != me}
    off = topo.mask(core, cores[plane[me][0]])
    chip_mask = {c: topo.mask(core, hop[c]) & ~off for c in hop if same_chip(topo, core, hop[c])}
    mask = {c: chip_mask.get(c, off) for c in hop}
    assert all(bits(m) == bits(off) for m in mask.values())
    E = bits(off)
    parts = {c: ("sA", "sB") if c in other[me] else ("s",) for c in hop}
    ns = sum(len(q) for q in parts.values())

    kind = len(other[me]) > len(plane[me])
    order1, order2 = [[me] + mix(p[kind], turn(plane[me], me, -1), turn(other[me], me, -1)) for p in TILES]
    events1, events2 = [steps(p[kind]) for p in TILES]
    arrive1, arrive2 = [mix(p[kind], turn(plane[me], me, 1), turn(other[me], me, 1)) for p in SUMS]

    def dst_id(k):
        rid, pid = topo.addr(k, core)
        return DstId(rid=rid, pnc=pid)

    on_list = [c for c in turn(other[me], me, 1) if c in chip_mask]
    off_list = [c for c in turn(other[me], me, 1) if c not in chip_mask] + turn(plane[me], me, 1)

    def cast_transfer(p, cs):
        v = piece(T, p, me, True)
        return RemoteDMATransfer(dst_ids=[dst_id(hop[c]) for c in cs], dma_engine_mask=mask[cs[0]],
                                 remote_sem=sem[p + str(me)], src=v, dsts=[v for c in cs])

    def send(p, c, lsem):
        rid, pid = topo.addr(hop[c], core)
        g.remote_dma(piece(T, p, me, False), piece(T, p, c, True), sem[p + str(me)], lsem, pid, rid, mask[c])

    groups = [cs for cs in (on_list, off_list) if cs]
    g.wait_ge(sem.qx, 1)
    for p in ("xp", "xc"):
        for cs in groups:
            g.remote_dma_fused([cast_transfer(p, cs)], local_sem=sem.lx)
    nx = 2 * len(groups) * E
    for e, k in events1:
        if e == "P" and k:
            g.wait_ge(sem.cv1, k + 1)
            g.wait_ge(sem.cs1, k + 1)
            for q in parts[order1[k]]:
                send(q, order1[k], sem.ls)
    g.wait_ge(sem.qh, 1)
    for p in ("hp", "hc"):
        g.remote_dma_fused([cast_transfer(p, cs) for cs in groups], local_sem=sem.lh)
    for e, k in events2:
        if e == "P" and k:
            g.wait_ge(sem.cs2, k + 1)
            send("y", order2[k], sem.ly)
    g.wait_ge(sem.ly, 5 * E)

    s = g.sync
    s.dma_start(T.xb[:], T.x[:]).then_inc(sem.ldx, 16)
    s.dma_start(T.w1b[:], T.w1[:]).then_inc(sem.ldw1, 16)
    s.dma_start(T.w2b[:], T.w2[:]).then_inc(sem.ldw2, 16)
    s.wait_ge(sem.lx, nx)
    s.dma_start(T.w3b[:], T.w3[:]).then_inc(sem.ldw34, 16)
    s.dma_start(T.w4b[:], T.w4[:]).then_inc(sem.ldw34, 16)
    s.wait_ge(sem.qt, 1)
    s.dma_start(T.t[me], slot(T.tb, me, 512)).then_inc(sem.st, 16)
    s.wait_ge(sem.qt, N)
    s.wait_ge(sem.ls, ns * E)
    for c in order1[1:]:
        s.dma_start(T.t[c], slot(T.tb, c, 512)).then_inc(sem.st, 16)
    s.wait_ge(sem.qh, 1)
    s.wait_ge(sem.lh, nx)
    s.dma_start(T.h[:], T.hb[:]).then_inc(sem.st, 16)
    s.wait_ge(sem.vy, N - 1)
    s.dma_start(T.y[:], T.yacc[:]).then_inc(sem.st, 16)
    s.wait_ge(sem.st, 16 * (N + 2))

    t = g.tensor

    def bank(k, j):
        b = 512 * (4 * (k % 2) + j)
        return T.ps[:, b:b + 128]

    def mm(out, w, i, x, c):
        return t.matmul_mx(out, T[w + "c"][:, 128 * i:128 * i + 128], T[w + "p"][:, 128 * i:128 * i + 128],
                           T[x + "c"][:, 128 * c:128 * c + 128], T[x + "p"][:, 128 * c:128 * c + 128], True, True)

    t.wait_ge(sem.qw1, 1)
    for e, k in events1:
        c = order1[k]
        if e == "Z":
            if k == 0:
                t.wait_ge(sem.qx, 1)
            else:
                t.wait_ge(sem["xp%d" % c], E)
                t.wait_ge(sem["xc%d" % c], E)
            mm(bank(k, 1), "w1", 1, "x", c).then_inc(sem.z1a, 1)
            mm(bank(k, 0), "w1", 0, "x", c).then_inc(sem.z0a, 1)
        else:
            if k == 0:
                t.wait_ge(sem.qw2, 1)
            t.wait_ge(sem.qt, k + 1)
            if k >= 2:
                t.wait_ge(sem.cv1, k - 1)
                t.wait_ge(sem.cs1, k - 1)
            mm(bank(k, 3), "w2", 1, "t", c).then_inc(sem.p1a, 1)
            mm(bank(k, 2), "w2", 0, "t", c).then_inc(sem.p0a, 1)
    t.wait_ge(sem.cv1, N)
    t.wait_ge(sem.cs1, N)
    t.wait_ge(sem.qw34, 2)
    for e, k in events2:
        c = order2[k]
        if e == "Z":
            if k == 0:
                t.wait_ge(sem.qh, 1)
            else:
                t.wait_ge(sem["hp%d" % c], E)
                t.wait_ge(sem["hc%d" % c], E)
            mm(bank(k, 1), "w3", 1, "h", c).then_inc(sem.z1b, 1)
            mm(bank(k, 0), "w3", 0, "h", c).then_inc(sem.z0b, 1)
        else:
            t.wait_ge(sem.qu, k + 1)
            if k >= 2:
                t.wait_ge(sem.cs2, k - 1)
            mm(bank(k, 2), "w4", 0, "u", c).then_inc(sem.p0b, 1)

    v = g.vector
    mx, mul = AluOpType.max, AluOpType.mult

    def quant(x, a, b, src):
        return v.quantize_mx(T[x + "c"][:, a:b], T[x + "p"][:, a:b], src)

    def v_acts(tile, c, k, z, va, sa, q, x):
        v.wait_ge(sem[z], k + 1)
        lo, hi = 512 * c, 512 * c + 512
        v.tensor_scalar(T[tile][:, lo:hi:4], bank(k, 0), 0.0, C1, mx, mul).then_inc(sem[va], 1)
        v.tensor_scalar(T[tile][:, lo + 1:hi:4], bank(k, 0), -C1, 0.0, mul, mx).then_inc(sem[va], 1)
        v.wait_ge(sem[va], 2 * k + 2)
        v.wait_ge(sem[sa], 2 * k + 2)
        quant(x, 128 * c, 128 * c + 128, T[tile][:, lo:hi]).then_inc(sem[q], 1)

    v.wait_ge(sem.ldx, 16)
    quant("x", 128 * me, 128 * me + 128, T.xb[:]).then_inc(sem.qx, 1)
    v.wait_ge(sem.ldw1, 16)
    quant("w1", 0, 256, T.w1b[:]).then_inc(sem.qw1, 1)
    v.wait_ge(sem.ldw2, 16)
    quant("w2", 0, 256, T.w2b[:]).then_inc(sem.qw2, 1)
    for e, k in events1:
        c = order1[k]
        if e == "Z":
            v_acts("tb", c, k, "z0a", "va1", "sa1", "qt", "t")
        else:
            v.wait_ge(sem.p0a, k + 1)
            v.tensor_copy(T.so[:, 256 * c:256 * c + 256:2], bank(k, 2)).then_inc(sem.cv1, 1)
    v.wait_ge(sem.ldw34, 32)
    quant("w3", 0, 256, T.w3b[:]).then_inc(sem.qw34, 1)
    quant("w4", 0, 128, T.w4b[:]).then_inc(sem.qw34, 1)
    v.wait_ge(sem.cv1, 1)
    v.wait_ge(sem.cs1, 1)
    n, last = 0, {0: 0, 128: 0}
    for r in arrive1:
        for q in parts[r]:
            lo, hi = CUT[q]
            v.wait_ge(sem[q + str(r)], E)
            need = max(last[b] for b in last if lo <= b < hi)
            if need:
                v.wait_ge(sem.va, need)
            own = T.acc[:, lo:hi] if need else T.so[:, 256 * me + lo:256 * me + hi]
            v.tensor_tensor(T.acc[:, lo:hi], own, T.sl[:, 256 * r + lo:256 * r + hi], AluOpType.add).then_inc(sem.va, 1)
            n += 1
            for b in last:
                if lo <= b < hi:
                    last[b] = n
    for b in last:
        v.wait_ge(sem.va, last[b])
        v.tensor_scalar(T.hb[:, 2 * b:2 * b + 256:2], T.acc[:, b:b + 128], 0.0, C2, mx, mul).then_inc(sem.vh, 1)
    v.wait_ge(sem.vh, 2)
    v.wait_ge(sem.sh, 2)
    quant("h", 128 * me, 128 * me + 128, T.hb[:]).then_inc(sem.qh, 1)
    for e, k in events2:
        if e == "Z":
            v_acts("ub", order2[k], k, "z0b", "va2", "sa2", "qu", "u")
    v.wait_ge(sem.cs2, 1)
    for i, r in enumerate(arrive2):
        v.wait_ge(sem["y%d" % r], E)
        if i:
            v.wait_ge(sem.vy, i)
        v.tensor_tensor(T.yacc[:], slot(T.yo, me, 128) if i == 0 else T.yacc[:], slot(T.yl, r, 128),
                        AluOpType.add).then_inc(sem.vy, 1)

    a = g.scalar
    relu, cp = ActivationFunctionType.Relu, ActivationFunctionType.Copy

    def s_acts(tile, c, k, z, sa):
        lo, hi = 512 * c, 512 * c + 512
        a.wait_ge(sem[z], k + 1)
        a.activation(T[tile][:, lo + 2:hi:4], bank(k, 1), relu, scale=C1).then_inc(sem[sa], 1)
        a.activation(T[tile][:, lo + 3:hi:4], bank(k, 1), relu, scale=-C1).then_inc(sem[sa], 1)

    for e, k in events1:
        c = order1[k]
        if e == "Z":
            s_acts("tb", c, k, "z1a", "sa1")
        else:
            a.wait_ge(sem.p1a, k + 1)
            a.activation(T.so[:, 256 * c + 1:256 * c + 256:2], bank(k, 3), cp).then_inc(sem.cs1, 1)
    for b in last:
        a.wait_ge(sem.va, last[b])
        a.activation(T.hb[:, 2 * b + 1:2 * b + 256:2], T.acc[:, b:b + 128], relu, scale=-C2).then_inc(sem.sh, 1)
    for e, k in events2:
        c = order2[k]
        if e == "Z":
            s_acts("ub", c, k, "z1b", "sa2")
        else:
            a.wait_ge(sem.p0b, k + 1)
            a.activation(slot(T.yo, c, 128), bank(k, 2), cp).then_inc(sem.cs2, 1)
